import numpy as np
import ml_dtypes


def mxq(x, axis, fmt="e4m3"):
    dtype, down = {"e4m3": (ml_dtypes.float8_e4m3fn, 7), "e5m2": (ml_dtypes.float8_e5m2, 14)}[fmt]
    v = np.moveaxis(np.asarray(x, np.float32).astype(ml_dtypes.bfloat16).astype(np.float64), axis, -1)
    blocks = v.reshape(v.shape[:-1] + (-1, 32))
    amax = np.abs(blocks).max(-1, keepdims=True)
    byte = np.maximum(np.where(amax > 0, np.frexp(amax)[1] - 1 + 127, 0) - down, 1)
    scale = np.exp2(byte - 127.0)
    codes = (blocks / scale).astype(np.float32).astype(dtype).astype(np.float64)
    return np.moveaxis((codes * scale).reshape(v.shape), -1, axis)


WIDE = False


def mx_kscale(k):
    if not WIDE:
        return np.ones(k)
    levels = np.array([10, -10, 5, -5, 0])
    if k % 512:
        return np.exp2(np.random.permutation(np.resize(levels, k // 32))).repeat(32)
    a = np.empty((k // 512, 16))
    for p in range(k // 512):
        a[p, :8] = np.random.permutation(np.resize(levels, 8))
        for g in range(8):
            far = levels[np.abs(levels - a[p, g]) >= 10]
            a[p, g + 8] = far[np.random.randint(len(far))]
    return np.exp2(a.ravel()).repeat(32)


BF16 = ml_dtypes.bfloat16


def bf(x):
    return np.asarray(x, np.float32).astype(BF16)


def f64(x):
    return np.asarray(x).astype(np.float64)

def planes(Y):
    n, m = Y.shape
    b = f64(bf(Y)).reshape(n // 32, 32, m)
    amax = np.abs(b).max(1)
    byte = np.clip(np.where(amax > 0, np.frexp(amax)[1] - 1 + 127 - 7, 1), 1, 254)
    codes = (b * np.exp2(127.0 - byte)[:, None, :]).reshape(n, m).astype(np.float32).astype(ml_dtypes.float8_e4m3fn).view(np.uint8)
    words = codes.reshape(n // 512, 128, 4, m).transpose(0, 1, 3, 2)
    return np.ascontiguousarray(words), np.ascontiguousarray(byte.astype(np.uint8).reshape(n // 512, 16, m))


M, N, D = 1024, 1536, 1024

REC_GAIN, IN_GAIN, BIAS_GAIN, AMP_SPREAD = 0.6, 0.7, 0.3, 0.8


def setup_inputs():
    s = mx_kscale(N)
    t = mx_kscale(D)
    amp = np.exp(AMP_SPREAD * np.random.randn(N))
    h_prev = amp[:, None] * np.tanh(np.random.randn(N, M))
    x = np.random.randn(D, M)
    w_rec = REC_GAIN * np.random.randn(N, N) / np.sqrt(N)
    w_in = IN_GAIN * np.random.randn(N, D) / np.sqrt(D)
    bias = BIAS_GAIN * np.random.randn(N)
    return {
        "h_prev": bf(h_prev * s[:, None]),
        "x": bf(x * t[:, None]),
        "w_rec": bf(w_rec / s[None, :]),
        "w_in": bf(w_in / t[None, :]),
        "bias": bf(bias),
        "amp": bf(amp),
    }


def reference(h_prev, x, w_rec, w_in, bias, amp):
    rec = mxq(f64(w_rec), 1, "e4m3") @ mxq(f64(h_prev), 0, "e4m3")
    inp = mxq(f64(w_in), 1, "e4m3") @ mxq(f64(x), 0, "e4m3")
    y = f64(amp)[:, None] * np.tanh(rec + inp + f64(bias)[:, None])
    Y = y.reshape(N, M)
    words, scales = planes(Y)
    return y, words, scales

@@ -1,0 +1,296 @@
+from contextlib import ExitStack
+
+import concourse.mybir as mybir
+from concourse.masks import make_identity
+
+M, N, D = 1024, 1536, 1024
+FLOPS = 2 * N * (N + D) * M
+
+F32 = mybir.dt.float32
+BF16 = mybir.dt.bfloat16
+U32 = mybir.dt.uint32
+I32 = mybir.dt.int32
+U8 = mybir.dt.uint8
+FP8X4 = mybir.dt.float8_e4m3fn_x4
+ACT = mybir.ActivationFunctionType
+ALU = mybir.AluOpType
+
+P = 128
+PACK = 4
+KP = P * PACK
+HALF = 512
+GROUPS = N // KP
+REC_PASSES = N // KP
+PASSES = (N + D) // KP
+UNITS = GROUPS * PASSES
+SCALAR_COLS = 192
+LAST_WIDTHS = (256, 128, 128)
+W_LOADS = [(0, 0, 1), (0, 1, 1), (0, 2, 1), (0, 3, 1), (0, 4, 1),
+           (1, 0, 1), (1, 1, 2), (1, 3, 2), (2, 0, 3), (2, 3, 2)]
+
+
+def tile_tanh_recurrent_state_step_g2_kernel(tc, h_prev, x, w_rec, w_in, bias, amp, out_0, out_1, out_2):
+    nc = tc.nc
+    words_hbm = out_1.rearrange("g p m t -> g p (m t)").bitcast(I32)
+    scales_hbm = out_2.bitcast(I32)
+
+    with ExitStack() as ctx:
+        keep = ctx.enter_context(tc.tile_pool(name="keep", bufs=1))
+        stream = ctx.enter_context(tc.tile_pool(name="stream", bufs=2))
+        psum = ctx.enter_context(tc.psum_pool(name="psum", bufs=1))
+        ctx.enter_context(tc.manual_schedule())
+
+        ident = keep.tile([P, P], F32, name="ident")
+        warm_in = keep.tile([P, 1], F32, name="warm_in")
+        warm_out = keep.tile([P, 1], F32, name="warm_out")
+        bias_sb = keep.tile([P, GROUPS, PACK], BF16, name="bias_sb")
+        amp_sb = keep.tile([P, GROUPS, PACK], BF16, name="amp_sb")
+        y_scales = keep.tile([P, GROUPS, M], U8, name="y_scales", align_bytes=64)
+
+        w_raw = {}
+        w_turned = {}
+        w_grouped = {}
+        w_codes = {}
+        a_raw = {}
+        a_grouped = {}
+        a_codes = {}
+        acc = {}
+        y32 = {}
+        y16 = {}
+        y_codes = {}
+
+        def load_w(i):
+            g, c0, n = W_LOADS[i]
+            raw = keep.tile([P, PACK, n * KP], BF16, name="w_raw%d" % i)
+            rows = slice(g * KP, (g + 1) * KP)
+            if c0 < REC_PASSES:
+                src = w_rec[rows, c0 * KP:(c0 + n) * KP]
+            else:
+                src = w_in[rows, (c0 - REC_PASSES) * KP:(c0 - REC_PASSES + n) * KP]
+            nc.sync.dma_start(out=raw[:], in_=src.rearrange("(p t) k -> p t k", t=PACK))
+            for j in range(n):
+                w_raw[g * PASSES + c0 + j] = (raw, j, n)
+
+        def load_a(half, c):
+            raw = stream.tile([P, PACK, HALF], BF16, name="a_raw", bufs=6)
+            cols = slice(half * HALF, (half + 1) * HALF)
+            if c < REC_PASSES:
+                src = h_prev[c * KP:(c + 1) * KP, cols]
+            else:
+                src = x[(c - REC_PASSES) * KP:(c - REC_PASSES + 1) * KP, cols]
+            nc.sync.dma_start(out=raw[:], in_=src.rearrange("(p j) m -> p j m", j=PACK))
+            a_raw[half, c] = raw
+
+        def turn_w(u):
+            raw, j, n = w_raw[u]
+            words = raw[:].rearrange("p t k -> p (t k)").bitcast(F32)
+            for b in range(2):
+                bank = psum.tile([P, 2, 2, P], F32, name="turn", bufs=3)
+                for tt in range(2):
+                    first = ((2 * b + tt) * n + j) * (KP // 2)
+                    for e in range(2):
+                        nc.tensor.transpose(bank[:, tt, e, :], words[:, first + e:first + KP // 2:2], ident[:])
+                w_turned[u, b] = bank
+
+        def copy_w(u, b):
+            if b == 0:
+                w_grouped[u] = stream.tile([P, PACK * KP], BF16, name="w_grouped", bufs=3, align_bytes=64)
+            dst = w_grouped[u][:, b * 2 * KP:(b + 1) * 2 * KP].bitcast(F32)
+            nc.scalar.copy(out=dst.rearrange("p (t n e) -> p t n e", t=2, e=2),
+                           in_=w_turned[u, b][:].rearrange("p t e n -> p t n e"))
+
+        def quantize_w(u):
+            codes = keep.tile([P, KP], U32, name="w_codes%d" % u, align_bytes=64)
+            scales = keep.tile([P, KP], U8, name="w_scales%d" % u, align_bytes=64)
+            nc.vector.quantize_mx(out=codes[:].bitcast(FP8X4), scales=scales[:], in_=w_grouped[u][:])
+            w_codes[u] = (codes, scales)
+
+        def interleaved(dst, src, lo, hi):
+            return (dst[:, lo:hi, :].rearrange("p (c i) t -> p c t i", i=4),
+                    src[:, :, lo:hi].rearrange("p t (c i) -> p c t i", i=4))
+
+        def interleave_a_vector(half, c):
+            a_grouped[half, c] = stream.tile([P, HALF, PACK], BF16, name="a_grouped", bufs=2, align_bytes=64)
+            dst, src = interleaved(a_grouped[half, c], a_raw[half, c], SCALAR_COLS, HALF)
+            nc.vector.tensor_copy(out=dst, in_=src)
+
+        def interleave_a_scalar(half, c):
+            dst, src = interleaved(a_grouped[half, c], a_raw[half, c], 0, SCALAR_COLS)
+            nc.scalar.copy(out=dst, in_=src)
+
+        def interleave_a(half, c):
+            interleave_a_vector(half, c)
+            interleave_a_scalar(half, c)
+
+        def quantize_a(half, c):
+            codes = keep.tile([P, HALF], U32, name="a_codes%d_%d" % (half, c), align_bytes=64)
+            scales = keep.tile([P, HALF], U8, name="a_scales%d_%d" % (half, c), align_bytes=64)
+            nc.vector.quantize_mx(out=codes[:].bitcast(FP8X4), scales=scales[:],
+                                  in_=a_grouped[half, c][:].rearrange("p m t -> p (m t)"))
+            a_codes[half, c] = (codes, scales)
+
+        def multiply(piece, t, c):
+            g, m0, width = piece
+            if c == 0:
+                acc[piece, t] = psum.tile([P, width], F32, name="acc", bufs=5)
+            wc, ws = w_codes[g * PASSES + c]
+            ac, asc = a_codes[m0 // HALF, c]
+            n_cols = slice(t * P, (t + 1) * P)
+            m_cols = slice(m0 % HALF, m0 % HALF + width)
+            nc.tensor.matmul_mx(out=acc[piece, t][:], lhsT=wc[:, n_cols].bitcast(FP8X4), lhsT_scale=ws[:, n_cols],
+                                rhs=ac[:, m_cols].bitcast(FP8X4), rhs_scale=asc[:, m_cols],
+                                start=(c == 0), stop=(c == PASSES - 1))
+
+        def activate(piece, t):
+            g, m0, width = piece
+            if t == 0:
+                y32[piece] = stream.tile([P, PACK, width], F32, name="y32", bufs=5, align_bytes=64)
+            nc.scalar.activation(out=y32[piece][:, t, :], in_=acc[piece, t][:], func=ACT.Tanh,
+                                 bias=bias_sb[:, g, t:t + 1])
+
+        def amplify(piece, t):
+            g, m0, width = piece
+            nc.vector.tensor_scalar(out=y32[piece][:, t, :], in0=y32[piece][:, t, :], scalar1=amp_sb[:, g, t:t + 1],
+                                    scalar2=None, op0=ALU.mult)
+
+        def store_y(piece):
+            g, m0, width = piece
+            dst = out_0[g * KP:(g + 1) * KP, m0:m0 + width].rearrange("(p t) m -> p t m", t=PACK)
+            nc.sync.dma_start(out=dst, in_=y32[piece][:])
+
+        def interleave_y(piece):
+            g, m0, width = piece
+            y16[piece] = stream.tile([P, width, PACK], BF16, name="y16", bufs=2, align_bytes=64)
+            dst, src = interleaved(y16[piece], y32[piece], 0, width)
+            nc.vector.tensor_copy(out=dst, in_=src)
+
+        def quantize_y(piece):
+            g, m0, width = piece
+            y_codes[piece] = stream.tile([P, width], U32, name="y_codes", bufs=3, align_bytes=64)
+            nc.vector.quantize_mx(out=y_codes[piece][:].bitcast(FP8X4), scales=y_scales[:, g, m0:m0 + width],
+                                  in_=y16[piece][:].rearrange("p m t -> p (m t)"))
+
+        def store_words(piece):
+            g, m0, width = piece
+            nc.sync.dma_start(out=words_hbm[g, :, m0:m0 + width], in_=y_codes[piece][:].bitcast(I32))
+
+        def store_scales(engine, g0, g1):
+            for q in range(4):
+                engine.dma_start(out=scales_hbm[g0:g1, 4 * q:4 * q + 4, :].rearrange("g r w -> r g w"),
+                                 in_=y_scales[32 * q:32 * q + 4, g0:g1, :].bitcast(I32))
+
+        for c in range(PASSES):
+            load_w(c)
+            load_a(0, c)
+        nc.sync.dma_start(out=bias_sb[:], in_=bias.rearrange("(g p t) -> p g t", g=GROUPS, t=PACK))
+        nc.sync.dma_start(out=amp_sb[:], in_=amp.rearrange("(g p t) -> p g t", g=GROUPS, t=PACK))
+        load_w(5)
+        load_w(6)
+        load_w(7)
+        load_a(1, 0)
+        load_w(8)
+
+        make_identity(nc, ident[:])
+        nc.vector.memset(warm_in[:], 0.0)
+        nc.scalar.activation(out=warm_out[:], in_=warm_in[:], func=ACT.Tanh)
+
+        left = [(g, 0, HALF) for g in range(GROUPS)]
+        right = [(g, HALF, HALF) for g in range(GROUPS - 1)]
+        last = []
+        m0 = HALF
+        for width in LAST_WIDTHS:
+            last.append((GROUPS - 1, m0, width))
+            m0 += width
+
+        def weights(u):
+            turn_w(u)
+            copy_w(u, 0)
+            copy_w(u, 1)
+
+        def passes(u):
+            g, c = divmod(u, PASSES)
+            for t in range(PACK):
+                multiply(left[g], t, c)
+
+        weights(0)
+        interleave_a(0, 0)
+        quantize_w(0)
+        quantize_a(0, 0)
+        for c in range(1, PASSES):
+            weights(c)
+            passes(c - 1)
+            interleave_a(0, c)
+            quantize_w(c)
+            quantize_a(0, c)
+        load_a(1, 1)
+        load_w(9)
+        load_a(1, 2)
+        load_a(1, 3)
+        load_a(1, 4)
+        weights(5)
+        quantize_w(5)
+        weights(6)
+        passes(4)
+        quantize_w(6)
+
+        right_chunk_at = {7: 0, 9: 1, 11: 2, 12: 3, 13: 4}
+        for j in range(5, UNITS):
+            ahead = j + 2
+            done = left[j // PASSES - 1] if j % PASSES == 0 else None
+            if done is not None:
+                for t in range(3):
+                    activate(done, t)
+                    amplify(done, t)
+            if ahead < UNITS:
+                weights(ahead)
+            if done is not None:
+                activate(done, 3)
+            passes(j)
+            chunk = right_chunk_at.get(j)
+            if chunk is not None:
+                interleave_a(1, chunk)
+            if j == 6:
+                interleave_y(left[0])
+            if ahead < UNITS:
+                quantize_w(ahead)
+            if done is not None:
+                amplify(done, 3)
+                store_y(done)
+            if j == 13:
+                interleave_y(left[1])
+            if chunk is not None:
+                quantize_a(1, chunk)
+            if j == 6:
+                quantize_y(left[0])
+                store_words(left[0])
+            if j == 14:
+                quantize_y(left[1])
+                store_words(left[1])
+
+        pending = left[2]
+        first = True
+        for piece in right + last:
+            for t in range(PACK):
+                for c in range(PASSES):
+                    multiply(piece, t, c)
+                if first:
+                    for tt in range(PACK):
+                        activate(pending, tt)
+                        amplify(pending, tt)
+                    store_y(pending)
+                    first = False
+                activate(piece, t)
+                if t == 0:
+                    interleave_y(pending)
+                amplify(piece, t)
+                if t == 0:
+                    quantize_y(pending)
+                    store_words(pending)
+                    if pending == right[1]:
+                        store_scales(nc.sync, 0, 2)
+            store_y(piece)
+            pending = piece
+        interleave_y(pending)
+        quantize_y(pending)
+        store_words(pending)
+        store_scales(nc.scalar, 2, 3)

@@ -23,10 +23,17 @@ GROUPS = N // KP
 REC_PASSES = N // KP
 PASSES = (N + D) // KP
 UNITS = GROUPS * PASSES
-SCALAR_COLS = 192
-LAST_WIDTHS = (256, 128, 128)
-W_LOADS = [(0, 0, 1), (0, 1, 1), (0, 2, 1), (0, 3, 1), (0, 4, 1),
-           (1, 0, 1), (1, 1, 2), (1, 3, 2), (2, 0, 3), (2, 3, 2)]
+TAIL = ((0, 256), (256, 384), (384, 512))
+W_LOADS = [(0, 0, 1, 0, 2), (0, 0, 1, 2, 4), (0, 1, 1, 0, 4), (0, 2, 1, 0, 4), (0, 3, 1, 0, 4), (0, 4, 1, 0, 4), (1, 0, 1, 0, 4),
+           (1, 1, 1, 0, 4), (1, 2, 1, 0, 4), (1, 3, 2, 0, 4), (2, 0, 1, 0, 4), (2, 1, 2, 0, 4), (2, 3, 2, 0, 4)]
+LOAD_ORDER = "w w a w a w a w a w a w w w w a w w a w a a a"
+HALVED = (0,)
+SORTED_ON = range(6, 15)
+SHARE = {(1, c): 192 for c in range(5)}
+ACC_BANKS, TURN_BANKS = 5, 3
+TENSOR_ORDER = "t0 t1 m0 t2 m1 t3 m2 t4 m3 t5 m4 t6 t7 m5 t8 m6 t9 m7 t10 m8 t11 m9 t12 m10 t13 m11 t14 m12 m13 m14"
+SCALAR_ORDER = "c0 c1 c2 c3 c4 c5 a0 a1 c6 a2 c7 a3 c8 i5 c9 c10 i6 c11 a4 a5 a6 c12 i7 c13 c14 a7 i8 i9 a8 a9 a10 a11"
+VECTOR_ORDER = "h0 i0 h1 a0 i1 w1 a1 i2 a2 w2 i3 a3 w3 i4 w4 a4 s6 w5 s7 m0 s8 m1 w6 s9 m2 i5 w7 m3 s10 w8 y0 s11 w9 a5 s12 i6 w10 q0 s13 w11 a6 s14 i7 w12 i8 w13 a7 w14 i9 a8 a9 m4 m5 m6 m7 m8 y1 m9 m10 q1 m11"
 
 
 def tile_tanh_recurrent_state_step_g2_kernel(tc, h_prev, x, w_rec, w_in, bias, amp, out_0, out_1, out_2):
@@ -47,32 +54,28 @@ def tile_tanh_recurrent_state_step_g2_kernel(tc, h_prev, x, w_rec, w_in, bias, a
         amp_sb = keep.tile([P, GROUPS, PACK], BF16, name="amp_sb")
         y_scales = keep.tile([P, GROUPS, M], U8, name="y_scales", align_bytes=64)
 
-        w_raw = {}
-        w_turned = {}
-        w_grouped = {}
-        w_codes = {}
-        a_raw = {}
-        a_grouped = {}
-        a_codes = {}
-        acc = {}
-        y32 = {}
-        y16 = {}
-        y_codes = {}
+        w_raw, w_sorted, w_turned, w_grouped, w_codes = {}, {}, {}, {}, {}
+        a_raw, a_grouped, a_codes = {}, {}, {}
+        acc, y32, y16, y_codes = {}, {}, {}, {}
 
         def load_w(i):
-            g, c0, n = W_LOADS[i]
-            raw = keep.tile([P, PACK, n * KP], BF16, name="w_raw%d" % i)
+            g, c0, n, t0, t1 = W_LOADS[i]
+            raw = keep.tile([P, t1 - t0, n * KP], BF16, name="w_raw%d" % i)
             rows = slice(g * KP, (g + 1) * KP)
             if c0 < REC_PASSES:
                 src = w_rec[rows, c0 * KP:(c0 + n) * KP]
             else:
                 src = w_in[rows, (c0 - REC_PASSES) * KP:(c0 - REC_PASSES + n) * KP]
-            nc.sync.dma_start(out=raw[:], in_=src.rearrange("(p t) k -> p t k", t=PACK))
+            nc.sync.dma_start(out=raw[:], in_=src.rearrange("(p t) k -> p t k", t=PACK)[:, t0:t1, :])
+            words = raw[:].rearrange("p t k -> p (t k)").bitcast(F32)
+            words = words.rearrange("p (t j q e) -> p t j e q", t=t1 - t0, j=n, e=2)
             for j in range(n):
-                w_raw[g * PASSES + c0 + j] = (raw, j, n)
+                w_raw[g * PASSES + c0 + j] = words[:, :, j, :, :]
+                for b in range(t0 // 2, t1 // 2):
+                    w_raw[g * PASSES + c0 + j, b] = words[:, 2 * b - t0:2 * b - t0 + 2, j, :, :]
 
         def load_a(half, c):
-            raw = stream.tile([P, PACK, HALF], BF16, name="a_raw", bufs=6)
+            raw = stream.tile([P, PACK, HALF], BF16, name="a_raw", bufs=5)
             cols = slice(half * HALF, (half + 1) * HALF)
             if c < REC_PASSES:
                 src = h_prev[c * KP:(c + 1) * KP, cols]
@@ -81,46 +84,54 @@ def tile_tanh_recurrent_state_step_g2_kernel(tc, h_prev, x, w_rec, w_in, bias, a
             nc.sync.dma_start(out=raw[:], in_=src.rearrange("(p j) m -> p j m", j=PACK))
             a_raw[half, c] = raw
 
-        def turn_w(u):
-            raw, j, n = w_raw[u]
-            words = raw[:].rearrange("p t k -> p (t k)").bitcast(F32)
-            for b in range(2):
-                bank = psum.tile([P, 2, 2, P], F32, name="turn", bufs=3)
-                for tt in range(2):
-                    first = ((2 * b + tt) * n + j) * (KP // 2)
-                    for e in range(2):
-                        nc.tensor.transpose(bank[:, tt, e, :], words[:, first + e:first + KP // 2:2], ident[:])
-                w_turned[u, b] = bank
+        def sort_w(u):
+            w_sorted[u] = stream.tile([P, PACK, 2, P], F32, name="w_sorted", bufs=3)
+            nc.vector.tensor_copy(out=w_sorted[u][:], in_=w_raw[u])
+
+        def turn_w(u, b):
+            src = w_sorted[u][:, 2 * b:2 * b + 2, :, :] if u in SORTED_ON else w_raw[u, b]
+            bank = psum.tile([P, 2, 2, P], F32, name="turn", bufs=TURN_BANKS)
+            for tt in range(2):
+                for e in range(2):
+                    nc.tensor.transpose(bank[:, tt, e, :], src[:, tt, e, :], ident[:])
+            w_turned[u, b] = bank
 
         def copy_w(u, b):
-            if b == 0:
+            if u not in w_grouped:
                 w_grouped[u] = stream.tile([P, PACK * KP], BF16, name="w_grouped", bufs=3, align_bytes=64)
             dst = w_grouped[u][:, b * 2 * KP:(b + 1) * 2 * KP].bitcast(F32)
             nc.scalar.copy(out=dst.rearrange("p (t n e) -> p t n e", t=2, e=2),
                            in_=w_turned[u, b][:].rearrange("p t e n -> p t n e"))
 
-        def quantize_w(u):
-            codes = keep.tile([P, KP], U32, name="w_codes%d" % u, align_bytes=64)
-            scales = keep.tile([P, KP], U8, name="w_scales%d" % u, align_bytes=64)
-            nc.vector.quantize_mx(out=codes[:].bitcast(FP8X4), scales=scales[:], in_=w_grouped[u][:])
-            w_codes[u] = (codes, scales)
+        def quantize_w(u, b0, b1):
+            if u not in w_codes:
+                codes = keep.tile([P, KP], U32, name="w_codes%d" % u, align_bytes=64)
+                scales = keep.tile([P, KP], U8, name="w_scales%d" % u, align_bytes=64)
+                w_codes[u] = (codes, scales)
+            codes, scales = w_codes[u]
+            cols = slice(b0 * 2 * P, b1 * 2 * P)
+            nc.vector.quantize_mx(out=codes[:, cols].bitcast(FP8X4), scales=scales[:, cols],
+                                  in_=w_grouped[u][:, b0 * 2 * KP:b1 * 2 * KP])
+
+        def w_parts(u):
+            return ((0, 1), (1, 2)) if u in HALVED else ((0, 2),)
 
         def interleaved(dst, src, lo, hi):
             return (dst[:, lo:hi, :].rearrange("p (c i) t -> p c t i", i=4),
                     src[:, :, lo:hi].rearrange("p t (c i) -> p c t i", i=4))
 
-        def interleave_a_vector(half, c):
-            a_grouped[half, c] = stream.tile([P, HALF, PACK], BF16, name="a_grouped", bufs=2, align_bytes=64)
-            dst, src = interleaved(a_grouped[half, c], a_raw[half, c], SCALAR_COLS, HALF)
-            nc.vector.tensor_copy(out=dst, in_=src)
-
-        def interleave_a_scalar(half, c):
-            dst, src = interleaved(a_grouped[half, c], a_raw[half, c], 0, SCALAR_COLS)
-            nc.scalar.copy(out=dst, in_=src)
+        def grouped_a(half, c):
+            if (half, c) not in a_grouped:
+                a_grouped[half, c] = stream.tile([P, HALF, PACK], BF16, name="a_grouped", bufs=2, align_bytes=64)
+            return a_grouped[half, c]
 
         def interleave_a(half, c):
-            interleave_a_vector(half, c)
-            interleave_a_scalar(half, c)
+            dst, src = interleaved(grouped_a(half, c), a_raw[half, c], SHARE.get((half, c), 0), HALF)
+            nc.vector.tensor_copy(out=dst, in_=src)
+
+        def interleave_a_share(half, c):
+            dst, src = interleaved(grouped_a(half, c), a_raw[half, c], 0, SHARE[half, c])
+            nc.scalar.copy(out=dst, in_=src)
 
         def quantize_a(half, c):
             codes = keep.tile([P, HALF], U32, name="a_codes%d_%d" % (half, c), align_bytes=64)
@@ -129,168 +140,218 @@ def tile_tanh_recurrent_state_step_g2_kernel(tc, h_prev, x, w_rec, w_in, bias, a
                                   in_=a_grouped[half, c][:].rearrange("p m t -> p (m t)"))
             a_codes[half, c] = (codes, scales)
 
-        def multiply(piece, t, c):
-            g, m0, width = piece
+        def multiply(block, t, c, lo, hi):
+            g, half = block
             if c == 0:
-                acc[piece, t] = psum.tile([P, width], F32, name="acc", bufs=5)
+                acc[block, t, lo] = psum.tile([P, hi - lo], F32, name="acc", bufs=ACC_BANKS)
             wc, ws = w_codes[g * PASSES + c]
-            ac, asc = a_codes[m0 // HALF, c]
+            ac, asc = a_codes[half, c]
             n_cols = slice(t * P, (t + 1) * P)
-            m_cols = slice(m0 % HALF, m0 % HALF + width)
-            nc.tensor.matmul_mx(out=acc[piece, t][:], lhsT=wc[:, n_cols].bitcast(FP8X4), lhsT_scale=ws[:, n_cols],
-                                rhs=ac[:, m_cols].bitcast(FP8X4), rhs_scale=asc[:, m_cols],
+            nc.tensor.matmul_mx(out=acc[block, t, lo][:], lhsT=wc[:, n_cols].bitcast(FP8X4), lhsT_scale=ws[:, n_cols],
+                                rhs=ac[:, lo:hi].bitcast(FP8X4), rhs_scale=asc[:, lo:hi],
                                 start=(c == 0), stop=(c == PASSES - 1))
 
-        def activate(piece, t):
-            g, m0, width = piece
-            if t == 0:
-                y32[piece] = stream.tile([P, PACK, width], F32, name="y32", bufs=5, align_bytes=64)
-            nc.scalar.activation(out=y32[piece][:, t, :], in_=acc[piece, t][:], func=ACT.Tanh,
+        def activate(block, t, lo, hi):
+            g, half = block
+            if block not in y32:
+                y32[block] = stream.tile([P, PACK, HALF], F32, name="y32", bufs=5, align_bytes=64)
+            nc.scalar.activation(out=y32[block][:, t, lo:hi], in_=acc[block, t, lo][:], func=ACT.Tanh,
                                  bias=bias_sb[:, g, t:t + 1])
 
-        def amplify(piece, t):
-            g, m0, width = piece
-            nc.vector.tensor_scalar(out=y32[piece][:, t, :], in0=y32[piece][:, t, :], scalar1=amp_sb[:, g, t:t + 1],
-                                    scalar2=None, op0=ALU.mult)
+        def amplify(block, t, lo, hi):
+            g, half = block
+            nc.vector.tensor_scalar(out=y32[block][:, t, lo:hi], in0=y32[block][:, t, lo:hi],
+                                    scalar1=amp_sb[:, g, t:t + 1], scalar2=None, op0=ALU.mult)
 
-        def store_y(piece):
-            g, m0, width = piece
-            dst = out_0[g * KP:(g + 1) * KP, m0:m0 + width].rearrange("(p t) m -> p t m", t=PACK)
-            nc.sync.dma_start(out=dst, in_=y32[piece][:])
+        def store_y(block, t0, t1, lo, hi):
+            g, half = block
+            dst = out_0[g * KP:(g + 1) * KP, half * HALF + lo:half * HALF + hi].rearrange("(p t) m -> p t m", t=PACK)
+            nc.sync.dma_start(out=dst[:, t0:t1, :], in_=y32[block][:, t0:t1, lo:hi])
 
-        def interleave_y(piece):
-            g, m0, width = piece
-            y16[piece] = stream.tile([P, width, PACK], BF16, name="y16", bufs=2, align_bytes=64)
-            dst, src = interleaved(y16[piece], y32[piece], 0, width)
-            nc.vector.tensor_copy(out=dst, in_=src)
+        def interleave_y(block, lo, hi):
+            y16[block, lo] = stream.tile([P, hi - lo, PACK], BF16, name="y16", bufs=2, align_bytes=64)
+            nc.vector.tensor_copy(out=y16[block, lo][:].rearrange("p (c i) t -> p c t i", i=4),
+                                  in_=y32[block][:, :, lo:hi].rearrange("p t (c i) -> p c t i", i=4))
 
-        def quantize_y(piece):
-            g, m0, width = piece
-            y_codes[piece] = stream.tile([P, width], U32, name="y_codes", bufs=3, align_bytes=64)
-            nc.vector.quantize_mx(out=y_codes[piece][:].bitcast(FP8X4), scales=y_scales[:, g, m0:m0 + width],
-                                  in_=y16[piece][:].rearrange("p m t -> p (m t)"))
+        def quantize_y(block, lo, hi):
+            g, half = block
+            if block not in y_codes:
+                y_codes[block] = stream.tile([P, HALF], U32, name="y_codes", bufs=3, align_bytes=64)
+            nc.vector.quantize_mx(out=y_codes[block][:, lo:hi].bitcast(FP8X4),
+                                  scales=y_scales[:, g, half * HALF + lo:half * HALF + hi],
+                                  in_=y16[block, lo][:].rearrange("p m t -> p (m t)"))
 
-        def store_words(piece):
-            g, m0, width = piece
-            nc.sync.dma_start(out=words_hbm[g, :, m0:m0 + width], in_=y_codes[piece][:].bitcast(I32))
+        def store_words(block, lo, hi):
+            g, half = block
+            nc.sync.dma_start(out=words_hbm[g, :, half * HALF + lo:half * HALF + hi],
+                              in_=y_codes[block][:, lo:hi].bitcast(I32))
 
-        def store_scales(engine, g0, g1):
+        def store_scales(on_scalar, g0, g1):
+            engine = nc.scalar if on_scalar else nc.sync
             for q in range(4):
                 engine.dma_start(out=scales_hbm[g0:g1, 4 * q:4 * q + 4, :].rearrange("g r w -> r g w"),
                                  in_=y_scales[32 * q:32 * q + 4, g0:g1, :].bitcast(I32))
 
-        for c in range(PASSES):
-            load_w(c)
-            load_a(0, c)
-        nc.sync.dma_start(out=bias_sb[:], in_=bias.rearrange("(g p t) -> p g t", g=GROUPS, t=PACK))
-        nc.sync.dma_start(out=amp_sb[:], in_=amp.rearrange("(g p t) -> p g t", g=GROUPS, t=PACK))
-        load_w(5)
-        load_w(6)
-        load_w(7)
-        load_a(1, 0)
-        load_w(8)
+        def windows(block, t):
+            return TAIL if block == last_block and t >= 2 else ((0, HALF),)
+
+        def out_windows(block):
+            return TAIL if block == last_block else ((0, HALF),)
+
+        def covering(f, block, ts, lo, hi):
+            return [(f, block, t, a, b) for t in ts for a, b in windows(block, t) if a < hi and lo < b]
+
+        def load_of(u, b):
+            g, c = divmod(u, PASSES)
+            return [(load_w, i) for i, (lg, c0, n, t0, t1) in enumerate(W_LOADS)
+                    if lg == g and c0 <= c < c0 + n and t0 <= 2 * b < t1]
+
+        def needs(step):
+            f, args = step[0], step[1:]
+            if f is sort_w:
+                return load_of(args[0], 0)
+            if f is turn_w:
+                return [(sort_w, args[0])] if args[0] in SORTED_ON else load_of(*args)
+            if f is copy_w:
+                return [(turn_w,) + args]
+            if f is quantize_w:
+                return [(copy_w, args[0], b) for b in range(args[1], args[2])]
+            if f is interleave_a or f is interleave_a_share:
+                return [(load_a,) + args]
+            if f is quantize_a:
+                return [(interleave_a,) + args] + ([(interleave_a_share,) + args] if args in SHARE else [])
+            if f is multiply:
+                (g, half), c = args[0], args[2]
+                u = g * PASSES + c
+                return [(quantize_w, u, b0, b1) for b0, b1 in w_parts(u) if b0 <= args[1] // 2 < b1] + [(quantize_a, half, c)]
+            if f is activate:
+                return [(multiply, args[0], args[1], PASSES - 1, args[2], args[3])]
+            if f is amplify:
+                return [(activate,) + args]
+            if f is store_y:
+                return covering(amplify, args[0], range(args[1], args[2]), args[3], args[4])
+            if f is interleave_y:
+                return covering(amplify, args[0], range(PACK), args[1], args[2])
+            if f is quantize_y:
+                return [(interleave_y,) + args]
+            if f is store_words:
+                return [(quantize_y, args[0], a, b) for a, b in out_windows(args[0]) if a < args[2] and args[1] < b]
+            if f is store_scales:
+                return [(quantize_y, (g, half), a, b) for g in range(args[1], args[2]) for half in range(2)
+                        for a, b in out_windows((g, half))]
+            return []
 
         make_identity(nc, ident[:])
+        nc.gpsimd.dma_start(out=bias_sb[:], in_=bias.rearrange("(g p t) -> p g t", g=GROUPS, t=PACK))
+        nc.gpsimd.dma_start(out=amp_sb[:], in_=amp.rearrange("(g p t) -> p g t", g=GROUPS, t=PACK))
         nc.vector.memset(warm_in[:], 0.0)
         nc.scalar.activation(out=warm_out[:], in_=warm_in[:], func=ACT.Tanh)
 
-        left = [(g, 0, HALF) for g in range(GROUPS)]
-        right = [(g, HALF, HALF) for g in range(GROUPS - 1)]
-        last = []
-        m0 = HALF
-        for width in LAST_WIDTHS:
-            last.append((GROUPS - 1, m0, width))
-            m0 += width
+        left = [(g, 0) for g in range(GROUPS)]
+        right = [(g, 1) for g in range(GROUPS)]
+        last_block = right[2]
+        full = (0, HALF)
 
-        def weights(u):
-            turn_w(u)
-            copy_w(u, 0)
-            copy_w(u, 1)
+        def turns(u):
+            return [(turn_w, u, 0), (turn_w, u, 1)]
+
+        def copies(u):
+            return [(copy_w, u, 0), (copy_w, u, 1)]
 
         def passes(u):
             g, c = divmod(u, PASSES)
-            for t in range(PACK):
-                multiply(left[g], t, c)
+            return [(multiply, left[g], t, c) + full for t in range(PACK)]
 
-        weights(0)
-        interleave_a(0, 0)
-        quantize_w(0)
-        quantize_a(0, 0)
-        for c in range(1, PASSES):
-            weights(c)
-            passes(c - 1)
-            interleave_a(0, c)
-            quantize_w(c)
-            quantize_a(0, c)
-        load_a(1, 1)
-        load_w(9)
-        load_a(1, 2)
-        load_a(1, 3)
-        load_a(1, 4)
-        weights(5)
-        quantize_w(5)
-        weights(6)
-        passes(4)
-        quantize_w(6)
+        def chain(block, t, lo, hi):
+            return [(multiply, block, t, c, lo, hi) for c in range(PASSES)]
 
-        right_chunk_at = {7: 0, 9: 1, 11: 2, 12: 3, 13: 4}
-        for j in range(5, UNITS):
-            ahead = j + 2
-            done = left[j // PASSES - 1] if j % PASSES == 0 else None
-            if done is not None:
-                for t in range(3):
-                    activate(done, t)
-                    amplify(done, t)
-            if ahead < UNITS:
-                weights(ahead)
-            if done is not None:
-                activate(done, 3)
-            passes(j)
-            chunk = right_chunk_at.get(j)
-            if chunk is not None:
-                interleave_a(1, chunk)
-            if j == 6:
-                interleave_y(left[0])
-            if ahead < UNITS:
-                quantize_w(ahead)
-            if done is not None:
-                amplify(done, 3)
-                store_y(done)
-            if j == 13:
-                interleave_y(left[1])
-            if chunk is not None:
-                quantize_a(1, chunk)
-            if j == 6:
-                quantize_y(left[0])
-                store_words(left[0])
-            if j == 14:
-                quantize_y(left[1])
-                store_words(left[1])
-
+        sync_q = []
+        nw = na = 0
+        for kind in LOAD_ORDER.split():
+            if kind == "w":
+                sync_q.append((load_w, nw))
+                nw += 1
+            else:
+                sync_q.append((load_a,) + divmod(na, PASSES))
+                na += 1
+        for block in left[:2]:
+            sync_q += [(store_y, block, 0, PACK) + full, (store_words, block) + full]
+        sync_q += [(store_y, left[2], t, t + 1) + full for t in range(PACK)]
         pending = left[2]
-        first = True
-        for piece in right + last:
-            for t in range(PACK):
-                for c in range(PASSES):
-                    multiply(piece, t, c)
-                if first:
-                    for tt in range(PACK):
-                        activate(pending, tt)
-                        amplify(pending, tt)
-                    store_y(pending)
-                    first = False
-                activate(piece, t)
+        for block in right:
+            for t in range(PACK if block != last_block else 2):
+                sync_q.append((store_y, block, t, t + 1) + full)
                 if t == 0:
-                    interleave_y(pending)
-                amplify(piece, t)
+                    sync_q.append((store_words, pending) + full)
+            pending = block
+        sync_q += [(store_scales, False, 0, 2), (store_y, last_block, 2, 4, 0, 256), (store_y, last_block, 2, 4, 256, 512),
+                   (store_words, last_block, 0, 256), (store_words, last_block, 256, 512)]
+
+        tensor_q = []
+        for word in TENSOR_ORDER.split():
+            tensor_q += (turns if word[0] == "t" else passes)(int(word[1:]))
+        for block in right:
+            for t in range(PACK if block != last_block else 2):
+                tensor_q += chain(block, t, 0, HALF)
+        for lo, hi in TAIL:
+            tensor_q += chain(last_block, 2, lo, hi) + chain(last_block, 3, lo, hi)
+
+        scalar_q, vector_q = [], []
+        for word in SCALAR_ORDER.split():
+            n = int(word[1:])
+            if word[0] == "c":
+                scalar_q += copies(n)
+            elif word[0] == "i":
+                scalar_q.append((interleave_a_share,) + divmod(n, PASSES))
+            else:
+                scalar_q.append((activate, left[n // PACK], n % PACK) + full)
+        for word in VECTOR_ORDER.split():
+            n = int(word[1:])
+            if word[0] == "s":
+                vector_q.append((sort_w, n))
+            elif word[0] == "h":
+                vector_q.append((quantize_w, 0, n, n + 1))
+            elif word[0] == "w":
+                vector_q.append((quantize_w, n, 0, 2))
+            elif word[0] == "i":
+                vector_q.append((interleave_a,) + divmod(n, PASSES))
+            elif word[0] == "a":
+                vector_q.append((quantize_a,) + divmod(n, PASSES))
+            elif word[0] == "m":
+                vector_q.append((amplify, left[n // PACK], n % PACK) + full)
+            elif word[0] == "y":
+                vector_q.append((interleave_y, left[n]) + full)
+            else:
+                vector_q.append((quantize_y, left[n]) + full)
+        pending = left[2]
+        for block in right:
+            for t in range(PACK if block != last_block else 2):
+                scalar_q.append((activate, block, t) + full)
                 if t == 0:
-                    quantize_y(pending)
-                    store_words(pending)
-                    if pending == right[1]:
-                        store_scales(nc.sync, 0, 2)
-            store_y(piece)
-            pending = piece
-        interleave_y(pending)
-        quantize_y(pending)
-        store_words(pending)
-        store_scales(nc.scalar, 2, 3)
+                    vector_q.append((interleave_y, pending) + full)
+                vector_q.append((amplify, block, t) + full)
+                if t == 0:
+                    vector_q.append((quantize_y, pending) + full)
+            pending = block
+        for window in TAIL:
+            scalar_q += [(activate, last_block, t) + window for t in (2, 3)]
+        wide, mid, end = TAIL
+        vector_q += [(amplify, last_block, 2) + wide, (amplify, last_block, 3) + wide, (amplify, last_block, 2) + mid,
+                     (interleave_y, last_block) + wide, (amplify, last_block, 3) + mid, (amplify, last_block, 2) + end,
+                     (quantize_y, last_block) + wide, (amplify, last_block, 3) + end, (interleave_y, last_block) + mid,
+                     (interleave_y, last_block) + end, (quantize_y, last_block) + mid, (quantize_y, last_block) + end]
+        scalar_q.append((store_scales, True, 2, 3))
+
+
+        queues = [sync_q, tensor_q, scalar_q, vector_q]
+        heads = [0] * len(queues)
+        made = set()
+        while sum(heads) < sum(len(queue) for queue in queues):
+            before = sum(heads)
+            for i, queue in enumerate(queues):
+                while heads[i] < len(queue) and all(need in made for need in needs(queue[heads[i]])):
+                    step = queue[heads[i]]
+                    step[0](*step[1:])
+                    made.add(step)
+                    heads[i] += 1
+            assert sum(heads) > before

@@ -50,8 +50,8 @@ def tile_tanh_recurrent_state_step_g2_kernel(tc, h_prev, x, w_rec, w_in, bias, a
         ident = keep.tile([P, P], F32, name="ident")
         warm_in = keep.tile([P, 1], F32, name="warm_in")
         warm_out = keep.tile([P, 1], F32, name="warm_out")
-        bias_sb = keep.tile([P, GROUPS, PACK], BF16, name="bias_sb")
-        amp_sb = keep.tile([P, GROUPS, PACK], BF16, name="amp_sb")
+        vec_rows = keep.tile([P, KP], BF16, name="vec_rows")
+        vec_cols = keep.tile([P, 2, 2 * GROUPS], F32, name="vec_cols")
         y_scales = keep.tile([P, GROUPS, M], U8, name="y_scales", align_bytes=64)
 
         w_raw, w_sorted, w_turned, w_grouped, w_codes = {}, {}, {}, {}, {}
@@ -84,9 +84,23 @@ def tile_tanh_recurrent_state_step_g2_kernel(tc, h_prev, x, w_rec, w_in, bias, a
             nc.sync.dma_start(out=raw[:], in_=src.rearrange("(p j) m -> p j m", j=PACK))
             a_raw[half, c] = raw
 
+        def turn_vectors():
+            words = vec_rows[:].bitcast(F32)
+            bank = psum.tile([P, 2, 2, P], F32, name="turn", bufs=TURN_BANKS)
+            for e in range(2):
+                nc.tensor.transpose(bank[:, 0, e, :], words[:, e:KP // 2:2], ident[:])
+            w_turned["vectors"] = bank
+
+        def copy_vectors():
+            nc.scalar.copy(out=vec_cols[:], in_=w_turned["vectors"][:, 0, :, 0:2 * GROUPS])
+
+        def vector_column(row, t):
+            at = ((t // 2) * 2 * GROUPS + row) * 2 + t % 2
+            return vec_cols[:].rearrange("p e r -> p (e r)").bitcast(BF16)[:, at:at + 1]
+
         def sort_w(u):
             w_sorted[u] = stream.tile([P, PACK, 2, P], F32, name="w_sorted", bufs=3)
-            nc.vector.tensor_copy(out=w_sorted[u][:], in_=w_raw[u])
+            nc.vector.tensor_copy(out=w_sorted[u][:].rearrange("p t e q -> p t q e"), in_=w_raw[u].rearrange("p t e q -> p t q e"))
 
         def turn_w(u, b):
             src = w_sorted[u][:, 2 * b:2 * b + 2, :, :] if u in SORTED_ON else w_raw[u, b]
@@ -156,12 +170,12 @@ def tile_tanh_recurrent_state_step_g2_kernel(tc, h_prev, x, w_rec, w_in, bias, a
             if block not in y32:
                 y32[block] = stream.tile([P, PACK, HALF], F32, name="y32", bufs=5, align_bytes=64)
             nc.scalar.activation(out=y32[block][:, t, lo:hi], in_=acc[block, t, lo][:], func=ACT.Tanh,
-                                 bias=bias_sb[:, g, t:t + 1])
+                                 bias=vector_column(g, t))
 
         def amplify(block, t, lo, hi):
             g, half = block
             nc.vector.tensor_scalar(out=y32[block][:, t, lo:hi], in0=y32[block][:, t, lo:hi],
-                                    scalar1=amp_sb[:, g, t:t + 1], scalar2=None, op0=ALU.mult)
+                                    scalar1=vector_column(GROUPS + g, t), scalar2=None, op0=ALU.mult)
 
         def store_y(block, t0, t1, lo, hi):
             g, half = block
@@ -212,6 +226,8 @@ def tile_tanh_recurrent_state_step_g2_kernel(tc, h_prev, x, w_rec, w_in, bias, a
                 return load_of(args[0], 0)
             if f is turn_w:
                 return [(sort_w, args[0])] if args[0] in SORTED_ON else load_of(*args)
+            if f is copy_vectors:
+                return [(turn_vectors,)]
             if f is copy_w:
                 return [(turn_w,) + args]
             if f is quantize_w:
@@ -225,7 +241,7 @@ def tile_tanh_recurrent_state_step_g2_kernel(tc, h_prev, x, w_rec, w_in, bias, a
                 u = g * PASSES + c
                 return [(quantize_w, u, b0, b1) for b0, b1 in w_parts(u) if b0 <= args[1] // 2 < b1] + [(quantize_a, half, c)]
             if f is activate:
-                return [(multiply, args[0], args[1], PASSES - 1, args[2], args[3])]
+                return [(multiply, args[0], args[1], PASSES - 1, args[2], args[3]), (copy_vectors,)]
             if f is amplify:
                 return [(activate,) + args]
             if f is store_y:
@@ -242,8 +258,9 @@ def tile_tanh_recurrent_state_step_g2_kernel(tc, h_prev, x, w_rec, w_in, bias, a
             return []
 
         make_identity(nc, ident[:])
-        nc.gpsimd.dma_start(out=bias_sb[:], in_=bias.rearrange("(g p t) -> p g t", g=GROUPS, t=PACK))
-        nc.gpsimd.dma_start(out=amp_sb[:], in_=amp.rearrange("(g p t) -> p g t", g=GROUPS, t=PACK))
+        nc.vector.memset(vec_rows[:].bitcast(F32), 0.0)
+        nc.gpsimd.dma_start(out=vec_rows[0:GROUPS, :], in_=bias.rearrange("(g k) -> g k", g=GROUPS))
+        nc.gpsimd.dma_start(out=vec_rows[GROUPS:2 * GROUPS, :], in_=amp.rearrange("(g k) -> g k", g=GROUPS))
         nc.vector.memset(warm_in[:], 0.0)
         nc.scalar.activation(out=warm_out[:], in_=warm_in[:], func=ACT.Tanh)
 
@@ -290,6 +307,8 @@ def tile_tanh_recurrent_state_step_g2_kernel(tc, h_prev, x, w_rec, w_in, bias, a
         tensor_q = []
         for word in TENSOR_ORDER.split():
             tensor_q += (turns if word[0] == "t" else passes)(int(word[1:]))
+            if word == "t0":
+                tensor_q.append((turn_vectors,))
         for block in right:
             for t in range(PACK if block != last_block else 2):
                 tensor_q += chain(block, t, 0, HALF)
@@ -301,6 +320,8 @@ def tile_tanh_recurrent_state_step_g2_kernel(tc, h_prev, x, w_rec, w_in, bias, a
             n = int(word[1:])
             if word[0] == "c":
                 scalar_q += copies(n)
+                if n == 0:
+                    scalar_q.append((copy_vectors,))
             elif word[0] == "i":
                 scalar_q.append((interleave_a_share,) + divmod(n, PASSES))
             else:

@@ -26,7 +26,7 @@ UNITS = GROUPS * PASSES
 TAIL = ((0, 256), (256, 384), (384, 512))
 W_LOADS = [(0, 0, 1, 0, 2), (0, 0, 1, 2, 4), (0, 1, 1, 0, 4), (0, 2, 1, 0, 4), (0, 3, 1, 0, 4), (0, 4, 1, 0, 4), (1, 0, 1, 0, 4),
            (1, 1, 1, 0, 4), (1, 2, 1, 0, 4), (1, 3, 2, 0, 4), (2, 0, 1, 0, 4), (2, 1, 2, 0, 4), (2, 3, 2, 0, 4)]
-LOAD_ORDER = "w w a w a w a w a w a w w w w a w w a w a a a"
+LOAD_ORDER = "w w a b w a w a w a w a w w w w a w w a w a a a"
 HALVED = (0,)
 SORTED_ON = range(6, 15)
 SHARE = {(1, c): 192 for c in range(5)}
@@ -83,6 +83,10 @@ def tile_tanh_recurrent_state_step_g2_kernel(tc, h_prev, x, w_rec, w_in, bias, a
                 src = x[(c - REC_PASSES) * KP:(c - REC_PASSES + 1) * KP, cols]
             nc.sync.dma_start(out=raw[:], in_=src.rearrange("(p j) m -> p j m", j=PACK))
             a_raw[half, c] = raw
+
+        def load_vectors():
+            nc.sync.dma_start(out=vec_rows[0:GROUPS, :], in_=bias.rearrange("(g k) -> g k", g=GROUPS))
+            nc.sync.dma_start(out=vec_rows[GROUPS:2 * GROUPS, :], in_=amp.rearrange("(g k) -> g k", g=GROUPS))
 
         def turn_vectors():
             words = vec_rows[:].bitcast(F32)
@@ -226,6 +230,8 @@ def tile_tanh_recurrent_state_step_g2_kernel(tc, h_prev, x, w_rec, w_in, bias, a
                 return load_of(args[0], 0)
             if f is turn_w:
                 return [(sort_w, args[0])] if args[0] in SORTED_ON else load_of(*args)
+            if f is turn_vectors:
+                return [(load_vectors,)]
             if f is copy_vectors:
                 return [(turn_vectors,)]
             if f is copy_w:
@@ -259,8 +265,6 @@ def tile_tanh_recurrent_state_step_g2_kernel(tc, h_prev, x, w_rec, w_in, bias, a
 
         make_identity(nc, ident[:])
         nc.vector.memset(vec_rows[:].bitcast(F32), 0.0)
-        nc.gpsimd.dma_start(out=vec_rows[0:GROUPS, :], in_=bias.rearrange("(g k) -> g k", g=GROUPS))
-        nc.gpsimd.dma_start(out=vec_rows[GROUPS:2 * GROUPS, :], in_=amp.rearrange("(g k) -> g k", g=GROUPS))
         nc.vector.memset(warm_in[:], 0.0)
         nc.scalar.activation(out=warm_out[:], in_=warm_in[:], func=ACT.Tanh)
 
@@ -288,6 +292,8 @@ def tile_tanh_recurrent_state_step_g2_kernel(tc, h_prev, x, w_rec, w_in, bias, a
             if kind == "w":
                 sync_q.append((load_w, nw))
                 nw += 1
+            elif kind == "b":
+                sync_q.append((load_vectors,))
             else:
                 sync_q.append((load_a,) + divmod(na, PASSES))
                 na += 1

from contextlib import ExitStack

import concourse.mybir as mybir
from concourse.masks import make_identity

M, N, D = 1024, 1536, 1024
FLOPS = 2 * N * (N + D) * M

F32 = mybir.dt.float32
BF16 = mybir.dt.bfloat16
U32 = mybir.dt.uint32
I32 = mybir.dt.int32
U8 = mybir.dt.uint8
FP8X4 = mybir.dt.float8_e4m3fn_x4
ACT = mybir.ActivationFunctionType
ALU = mybir.AluOpType

P = 128
PACK = 4
KP = P * PACK
HALF = 512
GROUPS = N // KP
REC_PASSES = N // KP
PASSES = (N + D) // KP
UNITS = GROUPS * PASSES
TAIL = ((0, 256), (256, 384), (384, 512))
W_LOADS = [(0, 0, 1, 0, 2), (0, 0, 1, 2, 4), (0, 1, 1, 0, 4), (0, 2, 1, 0, 4), (0, 3, 1, 0, 4), (0, 4, 1, 0, 4), (1, 0, 1, 0, 4),
           (1, 1, 1, 0, 4), (1, 2, 1, 0, 4), (1, 3, 2, 0, 4), (2, 0, 1, 0, 4), (2, 1, 2, 0, 4), (2, 3, 2, 0, 4)]
LOAD_ORDER = "w w a b w a w a w a w a w w w w a w w a w a a a"
HALVED = (0,)
SORTED_ON = range(6, 15)
SHARE = {(1, c): 192 for c in range(5)}
ACC_BANKS, TURN_BANKS = 5, 3
TENSOR_ORDER = "t0 t1 m0 t2 m1 t3 m2 t4 m3 t5 m4 t6 t7 m5 t8 m6 t9 m7 t10 m8 t11 m9 t12 m10 t13 m11 t14 m12 m13 m14"
SCALAR_ORDER = "c0 c1 c2 c3 c4 c5 a0 a1 c6 a2 c7 a3 c8 i5 c9 c10 i6 c11 a4 a5 a6 c12 i7 c13 c14 a7 i8 i9 a8 a9 a10 a11"
VECTOR_ORDER = "h0 i0 h1 a0 i1 w1 a1 i2 a2 w2 i3 a3 w3 i4 w4 a4 s6 w5 s7 m0 s8 m1 w6 s9 m2 i5 w7 m3 s10 w8 y0 s11 w9 a5 s12 i6 w10 q0 s13 w11 a6 s14 i7 w12 i8 w13 a7 w14 i9 a8 a9 m4 m5 m6 m7 m8 y1 m9 m10 q1 m11"


def tile_tanh_recurrent_state_step_g2_kernel(tc, h_prev, x, w_rec, w_in, bias, amp, out_0, out_1, out_2):
    nc = tc.nc
    words_hbm = out_1.rearrange("g p m t -> g p (m t)").bitcast(I32)
    scales_hbm = out_2.bitcast(I32)

    with ExitStack() as ctx:
        keep = ctx.enter_context(tc.tile_pool(name="keep", bufs=1))
        stream = ctx.enter_context(tc.tile_pool(name="stream", bufs=2))
        psum = ctx.enter_context(tc.psum_pool(name="psum", bufs=1))
        ctx.enter_context(tc.manual_schedule())

        ident = keep.tile([P, P], F32, name="ident")
        warm_in = keep.tile([P, 1], F32, name="warm_in")
        warm_out = keep.tile([P, 1], F32, name="warm_out")
        vec_rows = keep.tile([P, KP], BF16, name="vec_rows")
        vec_cols = keep.tile([P, 2, 2 * GROUPS], F32, name="vec_cols")
        y_scales = keep.tile([P, GROUPS, M], U8, name="y_scales", align_bytes=64)

        w_raw, w_sorted, w_turned, w_grouped, w_codes = {}, {}, {}, {}, {}
        a_raw, a_grouped, a_codes = {}, {}, {}
        acc, y32, y16, y_codes = {}, {}, {}, {}

        def load_w(i):
            g, c0, n, t0, t1 = W_LOADS[i]
            raw = keep.tile([P, t1 - t0, n * KP], BF16, name="w_raw%d" % i)
            rows = slice(g * KP, (g + 1) * KP)
            if c0 < REC_PASSES:
                src = w_rec[rows, c0 * KP:(c0 + n) * KP]
            else:
                src = w_in[rows, (c0 - REC_PASSES) * KP:(c0 - REC_PASSES + n) * KP]
            nc.sync.dma_start(out=raw[:], in_=src.rearrange("(p t) k -> p t k", t=PACK)[:, t0:t1, :])
            words = raw[:].rearrange("p t k -> p (t k)").bitcast(F32)
            words = words.rearrange("p (t j q e) -> p t j e q", t=t1 - t0, j=n, e=2)
            for j in range(n):
                w_raw[g * PASSES + c0 + j] = words[:, :, j, :, :]
                for b in range(t0 // 2, t1 // 2):
                    w_raw[g * PASSES + c0 + j, b] = words[:, 2 * b - t0:2 * b - t0 + 2, j, :, :]

        def load_a(half, c):
            raw = stream.tile([P, PACK, HALF], BF16, name="a_raw", bufs=5)
            cols = slice(half * HALF, (half + 1) * HALF)
            if c < REC_PASSES:
                src = h_prev[c * KP:(c + 1) * KP, cols]
            else:
                src = x[(c - REC_PASSES) * KP:(c - REC_PASSES + 1) * KP, cols]
            nc.sync.dma_start(out=raw[:], in_=src.rearrange("(p j) m -> p j m", j=PACK))
            a_raw[half, c] = raw

        def load_vectors():
            nc.sync.dma_start(out=vec_rows[0:GROUPS, :], in_=bias.rearrange("(g k) -> g k", g=GROUPS))
            nc.sync.dma_start(out=vec_rows[GROUPS:2 * GROUPS, :], in_=amp.rearrange("(g k) -> g k", g=GROUPS))

        def turn_vectors():
            words = vec_rows[:].bitcast(F32)
            bank = psum.tile([P, 2, 2, P], F32, name="turn", bufs=TURN_BANKS)
            for e in range(2):
                nc.tensor.transpose(bank[:, 0, e, :], words[:, e:KP // 2:2], ident[:])
            w_turned["vectors"] = bank

        def copy_vectors():
            nc.scalar.copy(out=vec_cols[:], in_=w_turned["vectors"][:, 0, :, 0:2 * GROUPS])

        def vector_column(row, t):
            at = ((t // 2) * 2 * GROUPS + row) * 2 + t % 2
            return vec_cols[:].rearrange("p e r -> p (e r)").bitcast(BF16)[:, at:at + 1]

        def sort_w(u):
            w_sorted[u] = stream.tile([P, PACK, 2, P], F32, name="w_sorted", bufs=3)
            nc.vector.tensor_copy(out=w_sorted[u][:].rearrange("p t e q -> p t q e"), in_=w_raw[u].rearrange("p t e q -> p t q e"))

        def turn_w(u, b):
            src = w_sorted[u][:, 2 * b:2 * b + 2, :, :] if u in SORTED_ON else w_raw[u, b]
            bank = psum.tile([P, 2, 2, P], F32, name="turn", bufs=TURN_BANKS)
            for tt in range(2):
                for e in range(2):
                    nc.tensor.transpose(bank[:, tt, e, :], src[:, tt, e, :], ident[:])
            w_turned[u, b] = bank

        def copy_w(u, b):
            if u not in w_grouped:
                w_grouped[u] = stream.tile([P, PACK * KP], BF16, name="w_grouped", bufs=3, align_bytes=64)
            dst = w_grouped[u][:, b * 2 * KP:(b + 1) * 2 * KP].bitcast(F32)
            nc.scalar.copy(out=dst.rearrange("p (t n e) -> p t n e", t=2, e=2),
                           in_=w_turned[u, b][:].rearrange("p t e n -> p t n e"))

        def quantize_w(u, b0, b1):
            if u not in w_codes:
                codes = keep.tile([P, KP], U32, name="w_codes%d" % u, align_bytes=64)
                scales = keep.tile([P, KP], U8, name="w_scales%d" % u, align_bytes=64)
                w_codes[u] = (codes, scales)
            codes, scales = w_codes[u]
            cols = slice(b0 * 2 * P, b1 * 2 * P)
            nc.vector.quantize_mx(out=codes[:, cols].bitcast(FP8X4), scales=scales[:, cols],
                                  in_=w_grouped[u][:, b0 * 2 * KP:b1 * 2 * KP])

        def w_parts(u):
            return ((0, 1), (1, 2)) if u in HALVED else ((0, 2),)

        def interleaved(dst, src, lo, hi):
            return (dst[:, lo:hi, :].rearrange("p (c i) t -> p c t i", i=4),
                    src[:, :, lo:hi].rearrange("p t (c i) -> p c t i", i=4))

        def grouped_a(half, c):
            if (half, c) not in a_grouped:
                a_grouped[half, c] = stream.tile([P, HALF, PACK], BF16, name="a_grouped", bufs=2, align_bytes=64)
            return a_grouped[half, c]

        def interleave_a(half, c):
            dst, src = interleaved(grouped_a(half, c), a_raw[half, c], SHARE.get((half, c), 0), HALF)
            nc.vector.tensor_copy(out=dst, in_=src)

        def interleave_a_share(half, c):
            dst, src = interleaved(grouped_a(half, c), a_raw[half, c], 0, SHARE[half, c])
            nc.scalar.copy(out=dst, in_=src)

        def quantize_a(half, c):
            codes = keep.tile([P, HALF], U32, name="a_codes%d_%d" % (half, c), align_bytes=64)
            scales = keep.tile([P, HALF], U8, name="a_scales%d_%d" % (half, c), align_bytes=64)
            nc.vector.quantize_mx(out=codes[:].bitcast(FP8X4), scales=scales[:],
                                  in_=a_grouped[half, c][:].rearrange("p m t -> p (m t)"))
            a_codes[half, c] = (codes, scales)

        def multiply(block, t, c, lo, hi):
            g, half = block
            if c == 0:
                acc[block, t, lo] = psum.tile([P, hi - lo], F32, name="acc", bufs=ACC_BANKS)
            wc, ws = w_codes[g * PASSES + c]
            ac, asc = a_codes[half, c]
            n_cols = slice(t * P, (t + 1) * P)
            nc.tensor.matmul_mx(out=acc[block, t, lo][:], lhsT=wc[:, n_cols].bitcast(FP8X4), lhsT_scale=ws[:, n_cols],
                                rhs=ac[:, lo:hi].bitcast(FP8X4), rhs_scale=asc[:, lo:hi],
                                start=(c == 0), stop=(c == PASSES - 1))

        def activate(block, t, lo, hi):
            g, half = block
            if block not in y32:
                y32[block] = stream.tile([P, PACK, HALF], F32, name="y32", bufs=5, align_bytes=64)
            nc.scalar.activation(out=y32[block][:, t, lo:hi], in_=acc[block, t, lo][:], func=ACT.Tanh,
                                 bias=vector_column(g, t))

        def amplify(block, t, lo, hi):
            g, half = block
            nc.vector.tensor_scalar(out=y32[block][:, t, lo:hi], in0=y32[block][:, t, lo:hi],
                                    scalar1=vector_column(GROUPS + g, t), scalar2=None, op0=ALU.mult)

        def store_y(block, t0, t1, lo, hi):
            g, half = block
            dst = out_0[g * KP:(g + 1) * KP, half * HALF + lo:half * HALF + hi].rearrange("(p t) m -> p t m", t=PACK)
            nc.sync.dma_start(out=dst[:, t0:t1, :], in_=y32[block][:, t0:t1, lo:hi])

        def interleave_y(block, lo, hi):
            y16[block, lo] = stream.tile([P, hi - lo, PACK], BF16, name="y16", bufs=2, align_bytes=64)
            nc.vector.tensor_copy(out=y16[block, lo][:].rearrange("p (c i) t -> p c t i", i=4),
                                  in_=y32[block][:, :, lo:hi].rearrange("p t (c i) -> p c t i", i=4))

        def quantize_y(block, lo, hi):
            g, half = block
            if block not in y_codes:
                y_codes[block] = stream.tile([P, HALF], U32, name="y_codes", bufs=3, align_bytes=64)
            nc.vector.quantize_mx(out=y_codes[block][:, lo:hi].bitcast(FP8X4),
                                  scales=y_scales[:, g, half * HALF + lo:half * HALF + hi],
                                  in_=y16[block, lo][:].rearrange("p m t -> p (m t)"))

        def store_words(block, lo, hi):
            g, half = block
            nc.sync.dma_start(out=words_hbm[g, :, half * HALF + lo:half * HALF + hi],
                              in_=y_codes[block][:, lo:hi].bitcast(I32))

        def store_scales(on_scalar, g0, g1):
            engine = nc.scalar if on_scalar else nc.sync
            for q in range(4):
                engine.dma_start(out=scales_hbm[g0:g1, 4 * q:4 * q + 4, :].rearrange("g r w -> r g w"),
                                 in_=y_scales[32 * q:32 * q + 4, g0:g1, :].bitcast(I32))

        def windows(block, t):
            return TAIL if block == last_block and t >= 2 else ((0, HALF),)

        def out_windows(block):
            return TAIL if block == last_block else ((0, HALF),)

        def covering(f, block, ts, lo, hi):
            return [(f, block, t, a, b) for t in ts for a, b in windows(block, t) if a < hi and lo < b]

        def load_of(u, b):
            g, c = divmod(u, PASSES)
            return [(load_w, i) for i, (lg, c0, n, t0, t1) in enumerate(W_LOADS)
                    if lg == g and c0 <= c < c0 + n and t0 <= 2 * b < t1]

        def needs(step):
            f, args = step[0], step[1:]
            if f is sort_w:
                return load_of(args[0], 0)
            if f is turn_w:
                return [(sort_w, args[0])] if args[0] in SORTED_ON else load_of(*args)
            if f is turn_vectors:
                return [(load_vectors,)]
            if f is copy_vectors:
                return [(turn_vectors,)]
            if f is copy_w:
                return [(turn_w,) + args]
            if f is quantize_w:
                return [(copy_w, args[0], b) for b in range(args[1], args[2])]
            if f is interleave_a or f is interleave_a_share:
                return [(load_a,) + args]
            if f is quantize_a:
                return [(interleave_a,) + args] + ([(interleave_a_share,) + args] if args in SHARE else [])
            if f is multiply:
                (g, half), c = args[0], args[2]
                u = g * PASSES + c
                return [(quantize_w, u, b0, b1) for b0, b1 in w_parts(u) if b0 <= args[1] // 2 < b1] + [(quantize_a, half, c)]
            if f is activate:
                return [(multiply, args[0], args[1], PASSES - 1, args[2], args[3]), (copy_vectors,)]
            if f is amplify:
                return [(activate,) + args]
            if f is store_y:
                return covering(amplify, args[0], range(args[1], args[2]), args[3], args[4])
            if f is interleave_y:
                return covering(amplify, args[0], range(PACK), args[1], args[2])
            if f is quantize_y:
                return [(interleave_y,) + args]
            if f is store_words:
                return [(quantize_y, args[0], a, b) for a, b in out_windows(args[0]) if a < args[2] and args[1] < b]
            if f is store_scales:
                return [(quantize_y, (g, half), a, b) for g in range(args[1], args[2]) for half in range(2)
                        for a, b in out_windows((g, half))]
            return []

        make_identity(nc, ident[:])
        nc.vector.memset(vec_rows[:].bitcast(F32), 0.0)
        nc.vector.memset(warm_in[:], 0.0)
        nc.scalar.activation(out=warm_out[:], in_=warm_in[:], func=ACT.Tanh)

        left = [(g, 0) for g in range(GROUPS)]
        right = [(g, 1) for g in range(GROUPS)]
        last_block = right[2]
        full = (0, HALF)

        def turns(u):
            return [(turn_w, u, 0), (turn_w, u, 1)]

        def copies(u):
            return [(copy_w, u, 0), (copy_w, u, 1)]

        def passes(u):
            g, c = divmod(u, PASSES)
            return [(multiply, left[g], t, c) + full for t in range(PACK)]

        def chain(block, t, lo, hi):
            return [(multiply, block, t, c, lo, hi) for c in range(PASSES)]

        sync_q = []
        nw = na = 0
        for kind in LOAD_ORDER.split():
            if kind == "w":
                sync_q.append((load_w, nw))
                nw += 1
            elif kind == "b":
                sync_q.append((load_vectors,))
            else:
                sync_q.append((load_a,) + divmod(na, PASSES))
                na += 1
        for block in left[:2]:
            sync_q += [(store_y, block, 0, PACK) + full, (store_words, block) + full]
        sync_q += [(store_y, left[2], t, t + 1) + full for t in range(PACK)]
        pending = left[2]
        for block in right:
            for t in range(PACK if block != last_block else 2):
                sync_q.append((store_y, block, t, t + 1) + full)
                if t == 0:
                    sync_q.append((store_words, pending) + full)
            pending = block
        sync_q += [(store_scales, False, 0, 2), (store_y, last_block, 2, 4, 0, 256), (store_y, last_block, 2, 4, 256, 512),
                   (store_words, last_block, 0, 256), (store_words, last_block, 256, 512)]

        tensor_q = []
        for word in TENSOR_ORDER.split():
            tensor_q += (turns if word[0] == "t" else passes)(int(word[1:]))
            if word == "t0":
                tensor_q.append((turn_vectors,))
        for block in right:
            for t in range(PACK if block != last_block else 2):
                tensor_q += chain(block, t, 0, HALF)
        for lo, hi in TAIL:
            tensor_q += chain(last_block, 2, lo, hi) + chain(last_block, 3, lo, hi)

        scalar_q, vector_q = [], []
        for word in SCALAR_ORDER.split():
            n = int(word[1:])
            if word[0] == "c":
                scalar_q += copies(n)
                if n == 0:
                    scalar_q.append((copy_vectors,))
            elif word[0] == "i":
                scalar_q.append((interleave_a_share,) + divmod(n, PASSES))
            else:
                scalar_q.append((activate, left[n // PACK], n % PACK) + full)
        for word in VECTOR_ORDER.split():
            n = int(word[1:])
            if word[0] == "s":
                vector_q.append((sort_w, n))
            elif word[0] == "h":
                vector_q.append((quantize_w, 0, n, n + 1))
            elif word[0] == "w":
                vector_q.append((quantize_w, n, 0, 2))
            elif word[0] == "i":
                vector_q.append((interleave_a,) + divmod(n, PASSES))
            elif word[0] == "a":
                vector_q.append((quantize_a,) + divmod(n, PASSES))
            elif word[0] == "m":
                vector_q.append((amplify, left[n // PACK], n % PACK) + full)
            elif word[0] == "y":
                vector_q.append((interleave_y, left[n]) + full)
            else:
                vector_q.append((quantize_y, left[n]) + full)
        pending = left[2]
        for block in right:
            for t in range(PACK if block != last_block else 2):
                scalar_q.append((activate, block, t) + full)
                if t == 0:
                    vector_q.append((interleave_y, pending) + full)
                vector_q.append((amplify, block, t) + full)
                if t == 0:
                    vector_q.append((quantize_y, pending) + full)
            pending = block
        for window in TAIL:
            scalar_q += [(activate, last_block, t) + window for t in (2, 3)]
        wide, mid, end = TAIL
        vector_q += [(amplify, last_block, 2) + wide, (amplify, last_block, 3) + wide, (amplify, last_block, 2) + mid,
                     (interleave_y, last_block) + wide, (amplify, last_block, 3) + mid, (amplify, last_block, 2) + end,
                     (quantize_y, last_block) + wide, (amplify, last_block, 3) + end, (interleave_y, last_block) + mid,
                     (interleave_y, last_block) + end, (quantize_y, last_block) + mid, (quantize_y, last_block) + end]
        scalar_q.append((store_scales, True, 2, 3))


        queues = [sync_q, tensor_q, scalar_q, vector_q]
        heads = [0] * len(queues)
        made = set()
        while sum(heads) < sum(len(queue) for queue in queues):
            before = sum(heads)
            for i, queue in enumerate(queues):
                while heads[i] < len(queue) and all(need in made for need in needs(queue[heads[i]])):
                    step = queue[heads[i]]
                    step[0](*step[1:])
                    made.add(step)
                    heads[i] += 1
            assert sum(heads) > before
